import numpy as np
import ml_dtypes


def mxq(x, axis, fmt="e4m3"):
    dtype, down = {"e4m3": (ml_dtypes.float8_e4m3fn, 7), "e5m2": (ml_dtypes.float8_e5m2, 14)}[fmt]
    v = np.moveaxis(np.asarray(x, np.float32).astype(ml_dtypes.bfloat16).astype(np.float64), axis, -1)
    blocks = v.reshape(v.shape[:-1] + (-1, 32))
    amax = np.abs(blocks).max(-1, keepdims=True)
    byte = np.maximum(np.where(amax > 0, np.frexp(amax)[1] - 1 + 127, 0) - down, 1)
    scale = np.exp2(byte - 127.0)
    codes = (blocks / scale).astype(np.float32).astype(dtype).astype(np.float64)
    return np.moveaxis((codes * scale).reshape(v.shape), -1, axis)


WIDE = False


def mx_kscale(k):
    if not WIDE:
        return np.ones(k)
    levels = np.array([10, -10, 5, -5, 0])
    if k % 512:
        return np.exp2(np.random.permutation(np.resize(levels, k // 32))).repeat(32)
    a = np.empty((k // 512, 16))
    for p in range(k // 512):
        a[p, :8] = np.random.permutation(np.resize(levels, 8))
        for g in range(8):
            far = levels[np.abs(levels - a[p, g]) >= 10]
            a[p, g + 8] = far[np.random.randint(len(far))]
    return np.exp2(a.ravel()).repeat(32)


def f64(x):
    return np.asarray(x).astype(np.float64)


def striped(idx):
    return np.tile(idx.reshape(-1, 16).T, (8, 1)).astype(np.uint16)


def unstriped(offs):
    return offs[:16].T.reshape(-1).astype(np.int64)


def striped8(idx):
    return np.concatenate([x.reshape(-1, 16).T for x in idx]).astype(np.uint16)


def runs(offs, k):
    lists = np.stack([offs[16 * r : 16 * r + 16].T.reshape(-1) for r in range(8)]).astype(np.int64)
    return lists[np.arange(k) % 512 // 64]


def pack_weight(w):
    k, n = w.shape
    w = f64(np.asarray(w, np.float32).astype(ml_dtypes.bfloat16)).reshape(k // 32, 32, n)
    amax = np.abs(w).max(1)
    byte = np.clip(np.where(amax > 0, np.frexp(amax)[1] - 1 + 127 - 7, 1), 1, 254)
    scaled = (w * np.exp2(127.0 - byte)[:, None, :]).reshape(k, n).astype(np.float32)
    words = np.ascontiguousarray(scaled.reshape(k // 512, 128, 4, n).transpose(0, 1, 3, 2)).astype(ml_dtypes.float8_e4m3fn).view(np.uint8)
    return words, np.ascontiguousarray(byte.astype(np.uint8).reshape(k // 512, 16, n))


def unpack_weight(words, scales):
    g, p, n, _ = words.shape
    vals = np.ascontiguousarray(words).view(ml_dtypes.float8_e4m3fn).astype(np.float64) * np.repeat(np.exp2(scales.astype(np.float64) - 127.0), 8, axis=1)[..., None]
    return vals.transpose(0, 1, 3, 2).reshape(g * 512, n)


def sigmoid(v):
    return 1.0 / (1.0 + np.exp(-np.maximum(v, -700.0)))


K, T, S, V, N, U, H = 512, 2048, 512, 1024, 512, 1024, 512


def setup_inputs():
    n = np.random.standard_normal
    s = mx_kscale(K)[:, None]
    u = mx_kscale(H)
    packed_xT = pack_weight(n((K, T)) * s)
    return {
        "x_words": packed_xT[0],
        "x_scales": packed_xT[1],
        "w1": (n((K, H)) / np.sqrt(K) / s * u).astype(np.float32),
        "w2": (n((K, H)) / np.sqrt(K) / s).astype(np.float32),
        "ma": (n((H, U)) * u[:, None]).astype(np.float32),
        "mb": n((H, U)).astype(np.float32),
        "w3": (n((H, N)) / np.sqrt(H) / u[:, None]).astype(np.float32),
        "offs": striped(np.random.permutation(T)[:S]),
        "two": striped(np.random.permutation(T)[:S]),
        "s1": striped8(np.stack([np.random.permutation(U)[:S] for _ in range(8)])),
        "s2": striped8(np.stack([np.random.permutation(U)[:S] for _ in range(8)])),
        "r1": striped8(np.stack([np.random.permutation(U) for _ in range(8)])),
        "r2": striped8(np.stack([np.random.permutation(U) for _ in range(8)])),
    }


def reference(x_words, x_scales, w1, w2, ma, mb, w3, offs, two, s1, s2, r1, r2):
    xq = unpack_weight(x_words, x_scales)[:, unstriped(offs)]
    y = mxq(f64(w1), 0, "e4m3").T @ xq
    pa = f64(ma).copy()
    pa[np.arange(H)[:, None], runs(s1, H)] = y
    x_two = unpack_weight(x_words, x_scales)[:, unstriped(two)]
    e = mxq(f64(w2), 0, "e4m3").T @ x_two
    pb = f64(mb).copy()
    pb[np.arange(H)[:, None], runs(s2, H)] = e
    z = (pa[np.arange(H)[:, None], runs(r1, H)]) * (sigmoid(pb[np.arange(H)[:, None], runs(r2, H)]))
    return mxq(f64(w3), 0, "e4m3").T @ mxq(z, 0, "e4m3")

@@ -1,0 +1,178 @@
+from contextlib import ExitStack
+
+import concourse.mybir as mybir
+
+K, T, S, V, N, U, H = 512, 2048, 512, 1024, 512, 1024, 512
+FLOPS = 2 * K * H * S * 2 + 2 * H * N * V
+
+F32 = mybir.dt.float32
+BF16 = mybir.dt.bfloat16
+I32 = mybir.dt.int32
+U32 = mybir.dt.uint32
+U16 = mybir.dt.uint16
+U8 = mybir.dt.uint8
+FP8X4 = mybir.dt.float8_e4m3fn_x4
+ACT = mybir.ActivationFunctionType
+MULT = mybir.AluOpType.mult
+
+P = 128
+PACK = 4
+LANES = 16
+CHUNK = 256
+
+
+def tile_picked_twopage_none_p_kernel(
+    tc, x_words, x_scales, w1, w2, ma, mb, w3, offs, two, s1, s2, r1, r2, out
+):
+    nc = tc.nc
+    with ExitStack() as ctx:
+        keep = ctx.enter_context(tc.tile_pool(name="keep", bufs=1))
+        psum = ctx.enter_context(tc.psum_pool(name="psum", bufs=8))
+
+        def load_list(src, name):
+            t = keep.tile(list(src.shape), U16, name=name)
+            nc.sync.dma_start(t[:], src)
+            return t
+
+        def load_weight(w, name):
+            raw = keep.tile([P, PACK, 512], F32, name=name, tag=name)
+            nc.sync.dma_start(raw[:], w.rearrange("(p j) c -> p j c", j=PACK))
+            return raw
+
+        def load_page(m, t, name):
+            page = keep.tile([P, U], F32, name=name)
+            nc.sync.dma_start(page[:], m.rearrange("(p t) u -> t p u", t=PACK)[t])
+            return page
+
+        two_l = load_list(two, "two_l")
+        xs = keep.tile([P, T], U8, name="xs", align_bytes=64)
+        for q in range(4):
+            rows = x_scales[0, 4 * q : 4 * q + 4, :].bitcast(I32)
+            nc.sync.dma_start(
+                xs[32 * q : 32 * q + 32, :].bitcast(I32),
+                rows.unsqueeze(0).broadcast_to([8, 4, T // 4]),
+            )
+        w2_raw = load_weight(w2, "w2_raw")
+        xw = keep.tile([P, T], I32, name="xw", align_bytes=64)
+        nc.sync.dma_start(xw[:], x_words[0].rearrange("p c r -> p (c r)").bitcast(I32))
+        offs_l = load_list(offs, "offs_l")
+        s2_l = load_list(s2, "s2_l")
+        pb = [load_page(mb, 0, "pb0")]
+        w1_raw = load_weight(w1, "w1_raw")
+        r2_l = load_list(r2, "r2_l")
+        pb.append(load_page(mb, 1, "pb1"))
+        pb.append(load_page(mb, 2, "pb2"))
+        w3_raw = load_weight(w3, "w3_raw")
+        pb.append(load_page(mb, 3, "pb3"))
+        s1_l = load_list(s1, "s1_l")
+        r1_l = load_list(r1, "r1_l")
+        pa = [load_page(ma, t, f"pa{t}") for t in range(PACK)]
+
+        def pick_scales(lst, name):
+            g = keep.tile([P, S], U8, name=name, align_bytes=64)
+            nc.vector.tensor_copy(g[:], xs[:].indirect(lst[:]))
+            return g
+
+        def pick_words(lst, name):
+            g = keep.tile([P, S], U32, name=name, align_bytes=64)
+            nc.vector.tensor_copy(g[:], xw[:].bitcast(U32).indirect(lst[:]))
+            return g
+
+        def round_dealt(raw, half, name):
+            g = keep.tile([P, 2 * P * PACK], BF16, name=name, align_bytes=64)
+            nc.scalar.copy(
+                g[:].rearrange("p (t m j) -> p m j t", t=2, j=PACK),
+                raw[:].rearrange("p j (m t) -> p m j t", t=PACK)[:, :, :, 2 * half : 2 * half + 2],
+            )
+            return g
+
+        def quantise(g, name, tag=None):
+            cols = g.shape[1] // PACK
+            codes = keep.tile([P, cols], U32, name=name + "_c", tag=tag or name + "_c", align_bytes=64)
+            scales = keep.tile([P, cols], U8, name=name + "_s", align_bytes=64)
+            nc.vector.quantize_mx(out=codes[:].bitcast(FP8X4), scales=scales[:], in_=g[:])
+            return codes, scales
+
+        def project(wq, i, xq, name):
+            acc = psum.tile([P, 512], F32, name="acc")
+            cols = slice(i * P, (i + 1) * P)
+            nc.tensor.matmul_mx(
+                out=acc[:],
+                lhsT=wq[0][:, cols].bitcast(FP8X4),
+                lhsT_scale=wq[1][:, cols],
+                rhs=xq[0][:].bitcast(FP8X4),
+                rhs_scale=xq[1][:],
+                start=True,
+                stop=True,
+            )
+            res = keep.tile([P, S], F32, name=name, tag=name, align_bytes=64)
+            nc.scalar.copy(res[:], acc[:])
+            return res
+
+        two_s = pick_scales(two_l, "two_s")
+        offs_s = pick_scales(offs_l, "offs_s")
+        w2_b = [round_dealt(w2_raw, h, f"w2_b{h}") for h in range(2)]
+        w2_q = [quantise(w2_b[h], f"w2_q{h}") for h in range(2)]
+        two_w = pick_words(two_l, "two_w")
+        offs_w = pick_words(offs_l, "offs_w")
+        e = [project(w2_q[t // 2], t % 2, (two_w, two_s), f"e{t}") for t in range(PACK)]
+        w1_b = [round_dealt(w1_raw, h, f"w1_b{h}") for h in range(2)]
+        w1_q = [quantise(w1_b[h], f"w1_q{h}") for h in range(2)]
+        y = [project(w1_q[t // 2], t % 2, (offs_w, offs_s), f"y{t}") for t in range(PACK)]
+
+        w3_b = keep.tile([P, N * PACK], BF16, name="w3_b", align_bytes=64)
+        nc.scalar.copy(
+            w3_b[:].rearrange("p (c i j) -> p c j i", i=2, j=PACK),
+            w3_raw[:].rearrange("p j (c i) -> p c j i", i=2),
+        )
+
+        chunks = V // CHUNK
+        gate = keep.tile([P, PACK, V], F32, name="gate", tag="w1_raw")
+        vals = [keep.tile([P, PACK, CHUNK], F32, name=f"vals{c}") for c in range(chunks)]
+
+        for t in range(PACK):
+            nc.vector.tensor_copy(pb[t][:].indirect(s2_l[:]), e[t][:])
+            for h in range(2):
+                part = r2_l[:, h * 32 : (h + 1) * 32]
+                nc.scalar.activation(gate[:, t, h * 512 : (h + 1) * 512], pb[t][:].indirect(part), ACT.Sigmoid)
+
+        for t in range(PACK):
+            nc.vector.tensor_copy(pa[t][:].indirect(s1_l[:]), y[t][:])
+            if t == 1:
+                w3_q = quantise(w3_b, "w3_q", tag="y1")
+            for c in range(chunks):
+                part = r1_l[:, c * CHUNK // LANES : (c + 1) * CHUNK // LANES]
+                nc.scalar.activation(vals[c][:, t, :], pa[t][:].indirect(part), ACT.Copy)
+
+        out_v = out.rearrange("(b p) v -> p b v", p=P)
+        spans = [(0, 256), (256, 256), (512, 256), (768, 128), (896, 128)]
+        for n, (v0, width) in enumerate(spans):
+            c, c0 = divmod(v0, CHUNK)
+            z = keep.tile([P, width * PACK], BF16, name=f"z{n}", align_bytes=64)
+            nc.vector.tensor_tensor(
+                z[:].rearrange("p (c i t) -> p c t i", i=2, t=PACK),
+                vals[c][:, :, c0 : c0 + width].rearrange("p t (c i) -> p c t i", i=2),
+                gate[:, :, v0 : v0 + width].rearrange("p t (c i) -> p c t i", i=2),
+                MULT,
+            )
+            zq = quantise(z, f"z_q{n}")
+            for h in range(2):
+                acc = psum.tile([P, 2 * width], F32, name="acc")
+                for i in range(2):
+                    cols = slice((2 * h + i) * P, (2 * h + i + 1) * P)
+                    nc.tensor.matmul_mx(
+                        out=acc[:, i * width : (i + 1) * width],
+                        lhsT=w3_q[0][:, cols].bitcast(FP8X4),
+                        lhsT_scale=w3_q[1][:, cols],
+                        rhs=zq[0][:].bitcast(FP8X4),
+                        rhs_scale=zq[1][:],
+                        start=True,
+                        stop=True,
+                    )
+                res = keep.tile([P, 2, width], F32, name=f"res{n}_{h}")
+                dst = res[:].rearrange("p b v -> p (b v)")
+                if n == len(spans) - 1 and h == 1:
+                    nc.vector.tensor_copy(dst, acc[:])
+                else:
+                    nc.scalar.copy(dst, acc[:])
+                nc.sync.dma_start(out_v[:, 2 * h : 2 * h + 2, v0 : v0 + width], res[:])

@@ -14,6 +14,7 @@ U8 = mybir.dt.uint8
 FP8X4 = mybir.dt.float8_e4m3fn_x4
 ACT = mybir.ActivationFunctionType
 MULT = mybir.AluOpType.mult
+ADD = mybir.AluOpType.add
 
 P = 128
 PACK = 4
@@ -45,6 +46,7 @@ def tile_picked_twopage_none_p_kernel(
             return page
 
         two_l = load_list(two, "two_l")
+        offs_l = load_list(offs, "offs_l")
         xs = keep.tile([P, T], U8, name="xs", align_bytes=64)
         for q in range(4):
             rows = x_scales[0, 4 * q : 4 * q + 4, :].bitcast(I32)
@@ -55,15 +57,17 @@ def tile_picked_twopage_none_p_kernel(
         w2_raw = load_weight(w2, "w2_raw")
         xw = keep.tile([P, T], I32, name="xw", align_bytes=64)
         nc.sync.dma_start(xw[:], x_words[0].rearrange("p c r -> p (c r)").bitcast(I32))
-        offs_l = load_list(offs, "offs_l")
         s2_l = load_list(s2, "s2_l")
         pb = [load_page(mb, 0, "pb0")]
         w1_raw = load_weight(w1, "w1_raw")
         r2_l = load_list(r2, "r2_l")
+        w3_raw = keep.tile([P, PACK, N], F32, name="w3_raw")
+        w3_rows = w3.rearrange("(p j) c -> p j c", j=PACK)
+        nc.sync.dma_start(w3_raw[:, 0:2, :], w3_rows[:, 0:2, :])
         pb.append(load_page(mb, 1, "pb1"))
-        pb.append(load_page(mb, 2, "pb2"))
-        w3_raw = load_weight(w3, "w3_raw")
-        pb.append(load_page(mb, 3, "pb3"))
+        nc.sync.dma_start(w3_raw[:, 2:4, :], w3_rows[:, 2:4, :])
+        for t in range(2, PACK):
+            pb.append(load_page(mb, t, f"pb{t}"))
         s1_l = load_list(s1, "s1_l")
         r1_l = load_list(r1, "r1_l")
         pa = [load_page(ma, t, f"pa{t}") for t in range(PACK)]
@@ -73,14 +77,17 @@ def tile_picked_twopage_none_p_kernel(
             nc.vector.tensor_copy(g[:], xs[:].indirect(lst[:]))
             return g
 
-        def pick_words(lst, name):
-            g = keep.tile([P, S], U32, name=name, align_bytes=64)
-            nc.vector.tensor_copy(g[:], xw[:].bitcast(U32).indirect(lst[:]))
+        def pick_words(lst, name, tag, parts):
+            g = keep.tile([P, S], U32, name=name, tag=tag, align_bytes=64)
+            step = S // parts
+            for s0 in range(0, S, step):
+                part = lst[:, s0 // LANES : (s0 + step) // LANES]
+                nc.vector.tensor_copy(g[:, s0 : s0 + step], xw[:].bitcast(U32).indirect(part))
             return g
 
-        def round_dealt(raw, half, name):
-            g = keep.tile([P, 2 * P * PACK], BF16, name=name, align_bytes=64)
-            nc.scalar.copy(
+        def round_dealt(raw, half, name, copy):
+            g = keep.tile([P, 2 * P * PACK], BF16, name=name, tag=name, align_bytes=64)
+            copy(
                 g[:].rearrange("p (t m j) -> p m j t", t=2, j=PACK),
                 raw[:].rearrange("p j (m t) -> p m j t", t=PACK)[:, :, :, 2 * half : 2 * half + 2],
             )
@@ -93,42 +100,45 @@ def tile_picked_twopage_none_p_kernel(
             nc.vector.quantize_mx(out=codes[:].bitcast(FP8X4), scales=scales[:], in_=g[:])
             return codes, scales
 
-        def project(wq, i, xq, name):
-            acc = psum.tile([P, 512], F32, name="acc")
-            cols = slice(i * P, (i + 1) * P)
-            nc.tensor.matmul_mx(
-                out=acc[:],
-                lhsT=wq[0][:, cols].bitcast(FP8X4),
-                lhsT_scale=wq[1][:, cols],
-                rhs=xq[0][:].bitcast(FP8X4),
-                rhs_scale=xq[1][:],
-                start=True,
-                stop=True,
-            )
+        def project(wq, i, xq, name, parts=1):
             res = keep.tile([P, S], F32, name=name, tag=name, align_bytes=64)
-            nc.scalar.copy(res[:], acc[:])
+            cols = slice(i * P, (i + 1) * P)
+            step = S // parts
+            for s0 in range(0, S, step):
+                acc = psum.tile([P, step], F32, name="acc")
+                nc.tensor.matmul_mx(
+                    out=acc[:],
+                    lhsT=wq[0][:, cols].bitcast(FP8X4),
+                    lhsT_scale=wq[1][:, cols],
+                    rhs=xq[0][:, s0 : s0 + step].bitcast(FP8X4),
+                    rhs_scale=xq[1][:, s0 : s0 + step],
+                    start=True,
+                    stop=True,
+                )
+                nc.scalar.copy(res[:, s0 : s0 + step], acc[:])
             return res
 
         two_s = pick_scales(two_l, "two_s")
         offs_s = pick_scales(offs_l, "offs_s")
-        w2_b = [round_dealt(w2_raw, h, f"w2_b{h}") for h in range(2)]
+        w2_b = [round_dealt(w2_raw, 0, "w2_b0", nc.vector.tensor_copy), round_dealt(w2_raw, 1, "w2_b1", nc.scalar.copy)]
         w2_q = [quantise(w2_b[h], f"w2_q{h}") for h in range(2)]
-        two_w = pick_words(two_l, "two_w")
-        offs_w = pick_words(offs_l, "offs_w")
-        e = [project(w2_q[t // 2], t % 2, (two_w, two_s), f"e{t}") for t in range(PACK)]
-        w1_b = [round_dealt(w1_raw, h, f"w1_b{h}") for h in range(2)]
+        two_w = pick_words(two_l, "two_w", "w2_b0", 2)
+        offs_w = pick_words(offs_l, "offs_w", "w2_b1", 1)
+        e = [project(w2_q[0], t, (two_w, two_s), f"e{t}", parts=2 - t) for t in range(2)]
+        w1_b = [round_dealt(w1_raw, h, f"w1_b{h}", nc.scalar.copy) for h in range(2)]
+        e.extend([project(w2_q[1], t, (two_w, two_s), f"e{2 + t}") for t in range(2)])
         w1_q = [quantise(w1_b[h], f"w1_q{h}") for h in range(2)]
         y = [project(w1_q[t // 2], t % 2, (offs_w, offs_s), f"y{t}") for t in range(PACK)]
 
-        w3_b = keep.tile([P, N * PACK], BF16, name="w3_b", align_bytes=64)
+        w3_b = keep.tile([P, N * PACK], BF16, name="w3_b", tag="w1_b1", align_bytes=64)
         nc.scalar.copy(
             w3_b[:].rearrange("p (c i j) -> p c j i", i=2, j=PACK),
             w3_raw[:].rearrange("p j (c i) -> p c j i", i=2),
         )
 
-        chunks = V // CHUNK
-        gate = keep.tile([P, PACK, V], F32, name="gate", tag="w1_raw")
-        vals = [keep.tile([P, PACK, CHUNK], F32, name=f"vals{c}") for c in range(chunks)]
+        gate = keep.tile([P, PACK, V], F32, name="gate", tag="w1_q1_c", align_bytes=64)
+        reads = [(0, 256), (256, 256), (512, 512)]
+        vals = [keep.tile([P, PACK, width], F32, name=f"vals{v0}") for v0, width in reads]
 
         for t in range(PACK):
             nc.vector.tensor_copy(pb[t][:].indirect(s2_l[:]), e[t][:])
@@ -138,16 +148,17 @@ def tile_picked_twopage_none_p_kernel(
 
         for t in range(PACK):
             nc.vector.tensor_copy(pa[t][:].indirect(s1_l[:]), y[t][:])
-            if t == 1:
-                w3_q = quantise(w3_b, "w3_q", tag="y1")
-            for c in range(chunks):
-                part = r1_l[:, c * CHUNK // LANES : (c + 1) * CHUNK // LANES]
+            if t == PACK - 1:
+                w3_q = quantise(w3_b, "w3_q", tag="y3")
+            for c, (v0, width) in enumerate(reads):
+                part = r1_l[:, v0 // LANES : (v0 + width) // LANES]
                 nc.scalar.activation(vals[c][:, t, :], pa[t][:].indirect(part), ACT.Copy)
 
         out_v = out.rearrange("(b p) v -> p b v", p=P)
-        spans = [(0, 256), (256, 256), (512, 256), (768, 128), (896, 128)]
+        spans = [(0, 128), (128, 128), (256, 256), (512, 256), (768, 128), (896, 128)]
         for n, (v0, width) in enumerate(spans):
-            c, c0 = divmod(v0, CHUNK)
+            c = min(v0 // CHUNK, len(reads) - 1)
+            c0 = v0 - reads[c][0]
             z = keep.tile([P, width * PACK], BF16, name=f"z{n}", align_bytes=64)
             nc.vector.tensor_tensor(
                 z[:].rearrange("p (c i t) -> p c t i", i=2, t=PACK),
@@ -171,7 +182,7 @@ def tile_picked_twopage_none_p_kernel(
                     )
                 res = keep.tile([P, 2, width], F32, name=f"res{n}_{h}")
                 dst = res[:].rearrange("p b v -> p (b v)")
-                if n == len(spans) - 1 and h == 1:
+                if n >= len(spans) - 2 and h == 1:
                     nc.vector.tensor_copy(dst, acc[:])
                 else:
                     nc.scalar.copy(dst, acc[:])

from contextlib import ExitStack

import concourse.mybir as mybir

K, T, S, V, N, U, H = 512, 2048, 512, 1024, 512, 1024, 512
FLOPS = 2 * K * H * S * 2 + 2 * H * N * V

F32 = mybir.dt.float32
BF16 = mybir.dt.bfloat16
I32 = mybir.dt.int32
U32 = mybir.dt.uint32
U16 = mybir.dt.uint16
U8 = mybir.dt.uint8
FP8X4 = mybir.dt.float8_e4m3fn_x4
ACT = mybir.ActivationFunctionType
MULT = mybir.AluOpType.mult
ADD = mybir.AluOpType.add

P = 128
PACK = 4
LANES = 16
CHUNK = 256


def tile_picked_twopage_none_p_kernel(
    tc, x_words, x_scales, w1, w2, ma, mb, w3, offs, two, s1, s2, r1, r2, out
):
    nc = tc.nc
    with ExitStack() as ctx:
        keep = ctx.enter_context(tc.tile_pool(name="keep", bufs=1))
        psum = ctx.enter_context(tc.psum_pool(name="psum", bufs=8))

        def load_list(src, name):
            t = keep.tile(list(src.shape), U16, name=name)
            nc.sync.dma_start(t[:], src)
            return t

        def load_weight(w, name):
            raw = keep.tile([P, PACK, 512], F32, name=name, tag=name)
            nc.sync.dma_start(raw[:], w.rearrange("(p j) c -> p j c", j=PACK))
            return raw

        def load_page(m, t, name):
            page = keep.tile([P, U], F32, name=name)
            nc.sync.dma_start(page[:], m.rearrange("(p t) u -> t p u", t=PACK)[t])
            return page

        two_l = load_list(two, "two_l")
        offs_l = load_list(offs, "offs_l")
        xs = keep.tile([P, T], U8, name="xs", align_bytes=64)
        for q in range(4):
            rows = x_scales[0, 4 * q : 4 * q + 4, :].bitcast(I32)
            nc.sync.dma_start(
                xs[32 * q : 32 * q + 32, :].bitcast(I32),
                rows.unsqueeze(0).broadcast_to([8, 4, T // 4]),
            )
        w2_raw = load_weight(w2, "w2_raw")
        xw = keep.tile([P, T], I32, name="xw", align_bytes=64)
        nc.sync.dma_start(xw[:], x_words[0].rearrange("p c r -> p (c r)").bitcast(I32))
        s2_l = load_list(s2, "s2_l")
        pb = [load_page(mb, 0, "pb0")]
        w1_raw = load_weight(w1, "w1_raw")
        r2_l = load_list(r2, "r2_l")
        w3_raw = keep.tile([P, PACK, N], F32, name="w3_raw")
        w3_rows = w3.rearrange("(p j) c -> p j c", j=PACK)
        nc.sync.dma_start(w3_raw[:, 0:2, :], w3_rows[:, 0:2, :])
        pb.append(load_page(mb, 1, "pb1"))
        nc.sync.dma_start(w3_raw[:, 2:4, :], w3_rows[:, 2:4, :])
        for t in range(2, PACK):
            pb.append(load_page(mb, t, f"pb{t}"))
        s1_l = load_list(s1, "s1_l")
        r1_l = load_list(r1, "r1_l")
        pa = [load_page(ma, t, f"pa{t}") for t in range(PACK)]

        def pick_scales(lst, name):
            g = keep.tile([P, S], U8, name=name, align_bytes=64)
            nc.vector.tensor_copy(g[:], xs[:].indirect(lst[:]))
            return g

        def pick_words(lst, name, tag, parts):
            g = keep.tile([P, S], U32, name=name, tag=tag, align_bytes=64)
            step = S // parts
            for s0 in range(0, S, step):
                part = lst[:, s0 // LANES : (s0 + step) // LANES]
                nc.vector.tensor_copy(g[:, s0 : s0 + step], xw[:].bitcast(U32).indirect(part))
            return g

        def round_dealt(raw, half, name, copy):
            g = keep.tile([P, 2 * P * PACK], BF16, name=name, tag=name, align_bytes=64)
            copy(
                g[:].rearrange("p (t m j) -> p m j t", t=2, j=PACK),
                raw[:].rearrange("p j (m t) -> p m j t", t=PACK)[:, :, :, 2 * half : 2 * half + 2],
            )
            return g

        def quantise(g, name, tag=None):
            cols = g.shape[1] // PACK
            codes = keep.tile([P, cols], U32, name=name + "_c", tag=tag or name + "_c", align_bytes=64)
            scales = keep.tile([P, cols], U8, name=name + "_s", align_bytes=64)
            nc.vector.quantize_mx(out=codes[:].bitcast(FP8X4), scales=scales[:], in_=g[:])
            return codes, scales

        def project(wq, i, xq, name, parts=1):
            res = keep.tile([P, S], F32, name=name, tag=name, align_bytes=64)
            cols = slice(i * P, (i + 1) * P)
            step = S // parts
            for s0 in range(0, S, step):
                acc = psum.tile([P, step], F32, name="acc")
                nc.tensor.matmul_mx(
                    out=acc[:],
                    lhsT=wq[0][:, cols].bitcast(FP8X4),
                    lhsT_scale=wq[1][:, cols],
                    rhs=xq[0][:, s0 : s0 + step].bitcast(FP8X4),
                    rhs_scale=xq[1][:, s0 : s0 + step],
                    start=True,
                    stop=True,
                )
                nc.scalar.copy(res[:, s0 : s0 + step], acc[:])
            return res

        two_s = pick_scales(two_l, "two_s")
        offs_s = pick_scales(offs_l, "offs_s")
        w2_b = [round_dealt(w2_raw, 0, "w2_b0", nc.vector.tensor_copy), round_dealt(w2_raw, 1, "w2_b1", nc.scalar.copy)]
        w2_q = [quantise(w2_b[h], f"w2_q{h}") for h in range(2)]
        two_w = pick_words(two_l, "two_w", "w2_b0", 2)
        offs_w = pick_words(offs_l, "offs_w", "w2_b1", 1)
        e = [project(w2_q[0], t, (two_w, two_s), f"e{t}", parts=2 - t) for t in range(2)]
        w1_b = [round_dealt(w1_raw, h, f"w1_b{h}", nc.scalar.copy) for h in range(2)]
        e.extend([project(w2_q[1], t, (two_w, two_s), f"e{2 + t}") for t in range(2)])
        w1_q = [quantise(w1_b[h], f"w1_q{h}") for h in range(2)]
        y = [project(w1_q[t // 2], t % 2, (offs_w, offs_s), f"y{t}") for t in range(PACK)]

        w3_b = keep.tile([P, N * PACK], BF16, name="w3_b", tag="w1_b1", align_bytes=64)
        nc.scalar.copy(
            w3_b[:].rearrange("p (c i j) -> p c j i", i=2, j=PACK),
            w3_raw[:].rearrange("p j (c i) -> p c j i", i=2),
        )

        gate = keep.tile([P, PACK, V], F32, name="gate", tag="w1_q1_c", align_bytes=64)
        reads = [(0, 256), (256, 256), (512, 512)]
        vals = [keep.tile([P, PACK, width], F32, name=f"vals{v0}") for v0, width in reads]

        for t in range(PACK):
            nc.vector.tensor_copy(pb[t][:].indirect(s2_l[:]), e[t][:])
            for h in range(2):
                part = r2_l[:, h * 32 : (h + 1) * 32]
                nc.scalar.activation(gate[:, t, h * 512 : (h + 1) * 512], pb[t][:].indirect(part), ACT.Sigmoid)

        for t in range(PACK):
            nc.vector.tensor_copy(pa[t][:].indirect(s1_l[:]), y[t][:])
            if t == PACK - 1:
                w3_q = quantise(w3_b, "w3_q", tag="y3")
            for c, (v0, width) in enumerate(reads):
                part = r1_l[:, v0 // LANES : (v0 + width) // LANES]
                nc.scalar.activation(vals[c][:, t, :], pa[t][:].indirect(part), ACT.Copy)

        out_v = out.rearrange("(b p) v -> p b v", p=P)
        spans = [(0, 128), (128, 128), (256, 256), (512, 256), (768, 128), (896, 128)]
        for n, (v0, width) in enumerate(spans):
            c = min(v0 // CHUNK, len(reads) - 1)
            c0 = v0 - reads[c][0]
            z = keep.tile([P, width * PACK], BF16, name=f"z{n}", align_bytes=64)
            nc.vector.tensor_tensor(
                z[:].rearrange("p (c i t) -> p c t i", i=2, t=PACK),
                vals[c][:, :, c0 : c0 + width].rearrange("p t (c i) -> p c t i", i=2),
                gate[:, :, v0 : v0 + width].rearrange("p t (c i) -> p c t i", i=2),
                MULT,
            )
            zq = quantise(z, f"z_q{n}")
            for h in range(2):
                acc = psum.tile([P, 2 * width], F32, name="acc")
                for i in range(2):
                    cols = slice((2 * h + i) * P, (2 * h + i + 1) * P)
                    nc.tensor.matmul_mx(
                        out=acc[:, i * width : (i + 1) * width],
                        lhsT=w3_q[0][:, cols].bitcast(FP8X4),
                        lhsT_scale=w3_q[1][:, cols],
                        rhs=zq[0][:].bitcast(FP8X4),
                        rhs_scale=zq[1][:],
                        start=True,
                        stop=True,
                    )
                res = keep.tile([P, 2, width], F32, name=f"res{n}_{h}")
                dst = res[:].rearrange("p b v -> p (b v)")
                if n >= len(spans) - 2 and h == 1:
                    nc.vector.tensor_copy(dst, acc[:])
                else:
                    nc.scalar.copy(dst, acc[:])
                nc.sync.dma_start(out_v[:, 2 * h : 2 * h + 2, v0 : v0 + width], res[:])
